import numpy as np
import ml_dtypes


def mxq(x, axis, fmt="e4m3"):
    dtype, down = {"e4m3": (ml_dtypes.float8_e4m3fn, 7), "e5m2": (ml_dtypes.float8_e5m2, 14)}[fmt]
    v = np.moveaxis(np.asarray(x, np.float32).astype(ml_dtypes.bfloat16).astype(np.float64), axis, -1)
    blocks = v.reshape(v.shape[:-1] + (-1, 32))
    amax = np.abs(blocks).max(-1, keepdims=True)
    byte = np.maximum(np.where(amax > 0, np.frexp(amax)[1] - 1 + 127, 0) - down, 1)
    scale = np.exp2(byte - 127.0)
    codes = (blocks / scale).astype(np.float32).astype(dtype).astype(np.float64)
    return np.moveaxis((codes * scale).reshape(v.shape), -1, axis)


WIDE = False


def mx_kscale(k):
    if not WIDE:
        return np.ones(k)
    levels = np.array([10, -10, 5, -5, 0])
    if k % 512:
        return np.exp2(np.random.permutation(np.resize(levels, k // 32))).repeat(32)
    a = np.empty((k // 512, 16))
    for p in range(k // 512):
        a[p, :8] = np.random.permutation(np.resize(levels, 8))
        for g in range(8):
            far = levels[np.abs(levels - a[p, g]) >= 10]
            a[p, g + 8] = far[np.random.randint(len(far))]
    return np.exp2(a.ravel()).repeat(32)


def f64(x):
    return np.asarray(x).astype(np.float64)


def striped(idx):
    return np.tile(np.asarray(idx).reshape(-1, 16).T, (8, 1)).astype(np.uint16)


def unstriped(offs):
    return offs[:16].T.reshape(-1).astype(np.int64)


E2M1 = np.array([0.0, 0.5, 1.0, 1.5, 2.0, 3.0, 4.0, 6.0, -0.0, -0.5, -1.0, -1.5, -2.0, -3.0, -4.0, -6.0])


def pack_weight(w, fmt):
    k, n = w.shape
    w = f64(np.asarray(w, np.float32).astype(ml_dtypes.bfloat16)).reshape(k // 32, 32, n)
    amax = np.abs(w).max(1)
    if fmt == "e4m3":
        byte = np.frexp(amax)[1] - 1 + 127 - 7
    else:
        mant, ex = np.frexp(amax / 6.0)
        byte = np.where(mant > 0.5, ex, ex - 1) + 127
    byte = np.clip(np.where(amax > 0, byte, 1), 1, 254)
    scaled = (w * np.exp2(127.0 - byte)[:, None, :]).reshape(k, n).astype(np.float32)
    by_word = np.ascontiguousarray(scaled.reshape(k // 512, 128, 4, n).transpose(0, 1, 3, 2))
    if fmt == "e4m3":
        words = by_word.astype(ml_dtypes.float8_e4m3fn).view(np.uint8)
    else:
        c = by_word.astype(ml_dtypes.float4_e2m1fn).view(np.uint8) & 0xF
        words = (c[..., 0::2] | (c[..., 1::2] << 4)).reshape(k // 512, 128, 2 * n)
    return np.ascontiguousarray(words), np.ascontiguousarray(byte.astype(np.uint8).reshape(k // 512, 16, n))


def unpack_weight(words, scales, fmt):
    g, _, n = scales.shape
    words = np.ascontiguousarray(words).reshape(g, 128, n, -1)
    if fmt == "e4m3":
        vals = words.view(ml_dtypes.float8_e4m3fn).astype(np.float64)
    else:
        nib = np.empty((g, 128, n, 4), np.uint8)
        nib[..., 0::2] = words & 0xF
        nib[..., 1::2] = words >> 4
        vals = E2M1[nib]
    vals = vals * np.repeat(np.exp2(scales.astype(np.float64) - 127.0), 8, axis=1)[..., None]
    return vals.transpose(0, 1, 3, 2).reshape(g * 512, n)


D, T, I, J, U, Z, M = 512, 2048, 512, 512, 1024, 1024, 1024


def setup_inputs():
    n = np.random.standard_normal
    idx = np.random.permutation(T)[:I]
    idx2 = np.random.permutation(U)[:J]
    idx3 = np.random.permutation(Z)[:J]
    idx4 = np.random.permutation(M)[:J]
    fd = mx_kscale(D)
    keysp = pack_weight(n((D, T)) / fd[:, None], "e4m3")
    return {
        "keys_words": keysp[0],
        "keys_scales": keysp[1],
        "notes": (n((D, U)) * 1.0 / np.sqrt(D) * fd[:, None]).astype(np.float32),
        "users2": (n((D, Z)) * 1.0 / np.sqrt(D) * fd[:, None]).astype(np.float32),
        "old": (1.0 * n((I, M))).astype(np.float32),
        "fade": (np.random.uniform(0.3, 0.9, (I, 1))).astype(np.float32),
        "offs": striped(idx),
        "offs2": striped(idx2),
        "offs3": striped(idx3),
        "offs4": striped(idx4),
    }


def reference(keys_words, keys_scales, notes, users2, old, fade, offs, offs2, offs3, offs4):
    idx = unstriped(offs)
    idx2 = unstriped(offs2)
    idx3 = unstriped(offs3)
    idx4 = unstriped(offs4)
    keysu = unpack_weight(keys_words, keys_scales, "e4m3")
    keysidxg = keysu[:, idx]
    notesidx2q = mxq(f64(notes)[:, idx2], 0, "e4m3")
    g1 = keysidxg.T @ notesidx2q
    users2idx3q = mxq(f64(users2)[:, idx3], 0, "e4m3")
    g2 = keysidxg.T @ users2idx3q
    g0 = np.maximum(g1, g2)
    gf = np.zeros((I, M))
    gf[:, idx4] = g0
    y = f64(old) * f64(fade) + gf
    return y

@@ -1,0 +1,205 @@
+from contextlib import ExitStack
+
+import concourse.mybir as mybir
+
+D, T, I, J, U, M = 512, 2048, 512, 512, 1024, 1024
+FLOPS = 2 * 2 * D * I * J
+
+F32 = mybir.dt.float32
+BF16 = mybir.dt.bfloat16
+I32 = mybir.dt.int32
+U32 = mybir.dt.uint32
+U16 = mybir.dt.uint16
+U8 = mybir.dt.uint8
+FP8X4 = mybir.dt.float8_e4m3fn_x4
+COPY = mybir.ActivationFunctionType.Copy
+ALU = mybir.AluOpType
+
+P = 128
+PACK = 4
+ROW_TILES = I // P
+HALF = J // 2
+PER_COL = 16
+
+
+def tile_attend_tab_larger_keep_kernel(tc, keys_words, keys_scales, notes, users2, old, fade, offs, offs2, offs3, offs4, out):
+    nc = tc.nc
+    with ExitStack() as ctx:
+        sb = ctx.enter_context(tc.tile_pool(name="sb", bufs=1))
+        reuse = ctx.enter_context(tc.tile_pool(name="reuse", bufs=1))
+        ps = ctx.enter_context(tc.psum_pool(name="ps", bufs=1))
+
+        def load_list(name, src):
+            t = sb.tile([P, src.shape[1]], U16, name=name)
+            nc.sync.dma_start(t[:], src)
+            return t
+
+        def entries(lst, first, count):
+            return lst[:, first // PER_COL : (first + count) // PER_COL]
+
+        def load_planes(name, table):
+            rows = table.rearrange("(p t) u -> t p u", t=PACK)
+            planes = []
+            for t in range(PACK):
+                plane = sb.tile([P, U], F32, name="%s_plane%d" % (name, t))
+                planes.append(plane)
+            return planes, rows
+
+        note_list = load_list("note_list", offs2)
+        key_list = load_list("key_list", offs)
+        user_list = load_list("user_list", offs3)
+        place_list = load_list("place_list", offs4)
+        note_planes, note_rows = load_planes("note", notes)
+        for h in range(2):
+            cols = slice(h * U // 2, (h + 1) * U // 2)
+            nc.sync.dma_start(note_planes[0][:, cols], note_rows[0][:, cols])
+        for t in (1, 2):
+            nc.sync.dma_start(note_planes[t][:], note_rows[t])
+        key_scale_pool = sb.tile([P, T], U8, name="key_scale_pool", align_bytes=64)
+        nc.gpsimd.memset(key_scale_pool[:].bitcast(I32), 0)
+        for q in range(4):
+            nc.sync.dma_start(
+                key_scale_pool[32 * q : 32 * q + 4, :].bitcast(I32),
+                keys_scales[0, 4 * q : 4 * q + 4, :].bitcast(I32),
+            )
+        nc.sync.dma_start(note_planes[3][:], note_rows[3])
+        key_word_pool = reuse.tile([P, T], I32, name="key_word_pool", align_bytes=64, offset=0)
+        nc.sync.dma_start(key_word_pool[:], keys_words[0].rearrange("p c r -> p (c r)").bitcast(I32))
+        user_planes, user_rows = load_planes("user", users2)
+        for t in range(PACK):
+            nc.sync.dma_start(user_planes[t][:], user_rows[t])
+        fade_sb = sb.tile([P, ROW_TILES], F32, name="fade_sb")
+        with nc.allow_non_contiguous_dma(reason="one value a row"):
+            nc.sync.dma_start(fade_sb[:], fade.rearrange("(r p) o -> p (r o)", p=P))
+        old_sb = []
+        for r in range(ROW_TILES):
+            t = sb.tile([P, M], F32, name="old%d" % r)
+            nc.sync.dma_start(t[:], old[r * P : (r + 1) * P, :])
+            old_sb.append(t)
+
+        placed = []
+        for r in range(ROW_TILES):
+            t = sb.tile([P, M], F32, name="placed%d" % r)
+            (nc.gpsimd if r < 2 else nc.vector).memset(t[:], 0.0)
+            placed.append(t)
+
+        def gather_and_weave(name, planes, lst, picked, on_scalar):
+            for t in range(PACK):
+                for h in (1, 0):
+                    window = planes[t][:].indirect(entries(lst, h * HALF, HALF))
+                    if (t, h) in on_scalar:
+                        nc.scalar.activation(picked[h][:, t, :], window, COPY)
+                    else:
+                        nc.vector.tensor_copy(picked[h][:, t, :], window)
+            woven = []
+            for h in range(2):
+                if name == "note" and h == 1:
+                    w = reuse.tile([P, HALF, PACK], BF16, name="note_woven1", align_bytes=64, offset=4 * T)
+                else:
+                    w = sb.tile([P, HALF, PACK], BF16, name="%s_woven%d" % (name, h), align_bytes=64)
+                dst = w[:].rearrange("p (c i) t -> p c t i", i=4)
+                src = picked[h][:].rearrange("p t (c i) -> p c t i", i=4)
+                if h == 0:
+                    nc.vector.tensor_copy(dst, src)
+                else:
+                    nc.scalar.copy(dst, src)
+                woven.append(w)
+            return woven
+
+        def quantise(codes, scales, woven):
+            nc.vector.quantize_mx(out=codes.bitcast(FP8X4), scales=scales, in_=woven[:].rearrange("p j t -> p (j t)"))
+
+        key_scales = sb.tile([P, I], U8, name="key_scales", align_bytes=64)
+        nc.vector.tensor_copy(key_scales[:], key_scale_pool[:].indirect(key_list[:]))
+        note_picked = [
+            sb.tile([P, PACK, HALF], BF16, name="note_picked0"),
+            sb.tile([P, PACK, HALF], BF16, name="note_picked1"),
+        ]
+        note_woven = gather_and_weave("note", note_planes, note_list, note_picked, [(t, 1) for t in range(PACK)])
+        note_codes = sb.tile([P, J], U32, name="note_codes", align_bytes=64)
+        note_scales = sb.tile([P, J], U8, name="note_scales", align_bytes=64)
+        for h in range(2):
+            cols = slice(h * HALF, (h + 1) * HALF)
+            quantise(note_codes[:, cols], note_scales[:, cols], note_woven[h])
+
+        key_words = sb.tile([P, I], U32, name="key_words", align_bytes=64)
+        nc.vector.tensor_copy(key_words[:], key_word_pool[:].bitcast(U32).indirect(key_list[:]))
+
+        def product(bank, r, codes, scales):
+            rows = slice(r * P, (r + 1) * P)
+            nc.tensor.matmul_mx(
+                out=bank, lhsT=key_words[:, rows].bitcast(FP8X4), lhsT_scale=key_scales[:, rows],
+                rhs=codes.bitcast(FP8X4), rhs_scale=scales, start=True, stop=True,
+            )
+
+        g1_banks = []
+        for r in range(ROW_TILES):
+            bank = ps.tile([P, J], F32, name="g1_bank%d" % r, tag="first%d" % r)
+            product(bank[:], r, note_codes[:], note_scales[:])
+            g1_banks.append(bank)
+
+        g1 = []
+        user_picked = [
+            reuse.tile([P, PACK, HALF], BF16, name="user_picked0", align_bytes=64, offset=4 * T - 1024),
+            reuse.tile([P, PACK, HALF], BF16, name="user_picked1", align_bytes=64, offset=4 * T + 1024),
+        ]
+        user_woven = gather_and_weave("user", user_planes, user_list, user_picked, [(0, 0), (0, 1), (3, 1)])
+        for r in range(ROW_TILES):
+            t = sb.tile([P, J], F32, name="g1_%d" % r)
+            nc.scalar.copy(t[:], g1_banks[r][:])
+            g1.append(t)
+
+        g0 = [sb.tile([P, J], F32, name="g0_%d" % r) for r in range(ROW_TILES)]
+        g2_banks = {}
+
+        def users_half(h):
+            codes = sb.tile([P, HALF], U32, name="user_codes%d" % h, align_bytes=64)
+            scales = sb.tile([P, HALF], U8, name="user_scales%d" % h, align_bytes=64)
+            quantise(codes[:], scales[:], user_woven[h])
+            for r in range(ROW_TILES):
+                bank = ps.tile([P, J], F32, name="g2_bank%d_%d" % (r, h), tag=("second%d" if h == 0 else "first%d") % r)
+                product(bank[:, :HALF], r, codes[:], scales[:])
+                g2_banks[(r, h)] = bank
+
+        def larger(r, h):
+            cols = slice(h * HALF, (h + 1) * HALF)
+            nc.vector.tensor_tensor(g0[r][:, cols], g2_banks[(r, h)][:, :HALF], g1[r][:, cols], ALU.max)
+
+        def place_vector(r, first, count):
+            nc.vector.tensor_copy(placed[r][:].indirect(entries(place_list, first, count)), g0[r][:, first : first + count])
+
+        def place_scalar(r, first, count):
+            nc.scalar.activation(placed[r][:].indirect(entries(place_list, first, count)), g0[r][:, first : first + count], COPY)
+
+        def finish(r, pieces):
+            width = M // pieces
+            for k in range(pieces):
+                cols = slice(k * width, (k + 1) * width)
+                nc.vector.scalar_tensor_tensor(
+                    out=old_sb[r][:, cols], in0=old_sb[r][:, cols], scalar=fade_sb[:, r : r + 1],
+                    in1=placed[r][:, cols], op0=ALU.mult, op1=ALU.add,
+                )
+                nc.sync.dma_start(out[r * P : (r + 1) * P, cols], old_sb[r][:, cols])
+
+        users_half(0)
+        larger(0, 0)
+        place_scalar(0, 0, HALF)
+        users_half(1)
+        larger(0, 1)
+        place_scalar(0, HALF, HALF)
+        larger(1, 0)
+        larger(1, 1)
+        place_scalar(1, 0, HALF)
+        place_scalar(1, HALF, HALF)
+        larger(3, 0)
+        larger(3, 1)
+        place_vector(3, 0, HALF)
+        larger(2, 0)
+        larger(2, 1)
+        place_vector(3, HALF, HALF)
+        place_vector(2, 384, 128)
+        place_scalar(2, 0, 384)
+        finish(0, 1)
+        finish(3, 1)
+        finish(1, 1)
+        finish(2, 2)

@@ -1,6 +1,7 @@
 from contextlib import ExitStack
 
 import concourse.mybir as mybir
+from concourse.masks import make_identity
 
 D, T, I, J, U, M = 512, 2048, 512, 512, 1024, 1024
 FLOPS = 2 * 2 * D * I * J
@@ -17,9 +18,20 @@ ALU = mybir.AluOpType
 
 P = 128
 PACK = 4
+QUADRANTS = 4
 ROW_TILES = I // P
 HALF = J // 2
-PER_COL = 16
+ENTRIES_PER_COLUMN = 16
+VECTOR_HALF, SCALAR_HALF = 0, 1
+
+LAST_TILE_ON_SCALAR = 384
+
+KIB = 1024
+KEY_WORDS_AT = 0
+NOTE_WOVEN_AT = 8 * KIB
+USER_PICKED_AT = 7 * KIB
+SCALAR_PICKED_AT = 11 * KIB
+LAST_PLANES_AT = 14 * KIB
 
 
 def tile_attend_tab_larger_keep_kernel(tc, keys_words, keys_scales, notes, users2, old, fade, offs, offs2, offs3, offs4, out):
@@ -29,93 +41,95 @@ def tile_attend_tab_larger_keep_kernel(tc, keys_words, keys_scales, notes, users
         reuse = ctx.enter_context(tc.tile_pool(name="reuse", bufs=1))
         ps = ctx.enter_context(tc.psum_pool(name="ps", bufs=1))
 
-        def load_list(name, src):
-            t = sb.tile([P, src.shape[1]], U16, name=name)
-            nc.sync.dma_start(t[:], src)
-            return t
+        def reused_tile(shape, dtype, name, offset):
+            return reuse.tile(shape, dtype, name=name, align_bytes=64, offset=offset)
 
-        def entries(lst, first, count):
-            return lst[:, first // PER_COL : (first + count) // PER_COL]
+        def load_list(name, source):
+            list_tile = sb.tile([P, source.shape[1]], U16, name=name)
+            nc.sync.dma_start(list_tile[:], source)
+            return list_tile
 
-        def load_planes(name, table):
-            rows = table.rearrange("(p t) u -> t p u", t=PACK)
-            planes = []
-            for t in range(PACK):
-                plane = sb.tile([P, U], F32, name="%s_plane%d" % (name, t))
-                planes.append(plane)
-            return planes, rows
+        def entries(list_tile, first, count):
+            return list_tile[:, first // ENTRIES_PER_COLUMN : (first + count) // ENTRIES_PER_COLUMN]
 
+        note_rows = notes.rearrange("(p t) u -> t p u", t=PACK)
+        note_planes = [sb.tile([P, U], F32, name="note_plane%d" % t) for t in range(PACK)]
+        for h in range(2):
+            cols = slice(h * U // 2, (h + 1) * U // 2)
+            nc.sync.dma_start(note_planes[0][:, cols], note_rows[0][:, cols])
         note_list = load_list("note_list", offs2)
         key_list = load_list("key_list", offs)
         user_list = load_list("user_list", offs3)
         place_list = load_list("place_list", offs4)
-        note_planes, note_rows = load_planes("note", notes)
-        for h in range(2):
-            cols = slice(h * U // 2, (h + 1) * U // 2)
-            nc.sync.dma_start(note_planes[0][:, cols], note_rows[0][:, cols])
         for t in (1, 2):
             nc.sync.dma_start(note_planes[t][:], note_rows[t])
+
         key_scale_pool = sb.tile([P, T], U8, name="key_scale_pool", align_bytes=64)
         nc.gpsimd.memset(key_scale_pool[:].bitcast(I32), 0)
-        for q in range(4):
+        for q in range(QUADRANTS):
             nc.sync.dma_start(
                 key_scale_pool[32 * q : 32 * q + 4, :].bitcast(I32),
                 keys_scales[0, 4 * q : 4 * q + 4, :].bitcast(I32),
             )
+        fade_rows = sb.tile([P, P], F32, name="fade_rows")
+        nc.gpsimd.memset(fade_rows[:], 0.0)
+        nc.sync.dma_start(fade_rows[0:ROW_TILES, :], fade.rearrange("(r p) o -> r (p o)", p=P))
         nc.sync.dma_start(note_planes[3][:], note_rows[3])
-        key_word_pool = reuse.tile([P, T], I32, name="key_word_pool", align_bytes=64, offset=0)
+
+        key_word_pool = reused_tile([P, T], I32, "key_word_pool", KEY_WORDS_AT)
         nc.sync.dma_start(key_word_pool[:], keys_words[0].rearrange("p c r -> p (c r)").bitcast(I32))
-        user_planes, user_rows = load_planes("user", users2)
+
+        user_rows = users2.rearrange("(p t) u -> t p u", t=PACK)
+        user_planes = [sb.tile([P, U], F32, name="user_plane%d" % t) for t in (0, 1)]
+        user_planes.extend(
+            reused_tile([P, U], F32, "user_plane%d" % t, LAST_PLANES_AT + (t - 2) * 4 * U) for t in (2, 3)
+        )
         for t in range(PACK):
             nc.sync.dma_start(user_planes[t][:], user_rows[t])
-        fade_sb = sb.tile([P, ROW_TILES], F32, name="fade_sb")
-        with nc.allow_non_contiguous_dma(reason="one value a row"):
-            nc.sync.dma_start(fade_sb[:], fade.rearrange("(r p) o -> p (r o)", p=P))
-        old_sb = []
-        for r in range(ROW_TILES):
-            t = sb.tile([P, M], F32, name="old%d" % r)
-            nc.sync.dma_start(t[:], old[r * P : (r + 1) * P, :])
-            old_sb.append(t)
 
-        placed = []
+        old_tiles = [sb.tile([P, M], F32, name="old%d" % r) for r in range(ROW_TILES)]
         for r in range(ROW_TILES):
-            t = sb.tile([P, M], F32, name="placed%d" % r)
-            (nc.gpsimd if r < 2 else nc.vector).memset(t[:], 0.0)
-            placed.append(t)
+            nc.sync.dma_start(old_tiles[r][:], old[r * P : (r + 1) * P, :])
 
-        def gather_and_weave(name, planes, lst, picked, on_scalar):
+        placed = [sb.tile([P, M], F32, name="placed%d" % r) for r in range(ROW_TILES)]
+        for r in range(ROW_TILES):
+            nc.vector.memset(placed[r][:].bitcast(I32), 0)
+
+        identity = sb.tile([P, P], F32, name="identity")
+        make_identity(nc, identity[:])
+        fade_bank = ps.tile([P, P], F32, name="fade_bank", tag="g2_3")
+        nc.tensor.transpose(fade_bank[:], fade_rows[:], identity[:])
+        fade_columns = sb.tile([P, ROW_TILES], F32, name="fade_columns")
+        nc.scalar.copy(fade_columns[:], fade_bank[:, :ROW_TILES])
+
+        def gather_planes(planes, list_tile, picked):
             for t in range(PACK):
-                for h in (1, 0):
-                    window = planes[t][:].indirect(entries(lst, h * HALF, HALF))
-                    if (t, h) in on_scalar:
-                        nc.scalar.activation(picked[h][:, t, :], window, COPY)
-                    else:
-                        nc.vector.tensor_copy(picked[h][:, t, :], window)
-            woven = []
-            for h in range(2):
-                if name == "note" and h == 1:
-                    w = reuse.tile([P, HALF, PACK], BF16, name="note_woven1", align_bytes=64, offset=4 * T)
-                else:
-                    w = sb.tile([P, HALF, PACK], BF16, name="%s_woven%d" % (name, h), align_bytes=64)
-                dst = w[:].rearrange("p (c i) t -> p c t i", i=4)
-                src = picked[h][:].rearrange("p t (c i) -> p c t i", i=4)
-                if h == 0:
-                    nc.vector.tensor_copy(dst, src)
-                else:
-                    nc.scalar.copy(dst, src)
-                woven.append(w)
-            return woven
+                window = planes[t][:]
+                scalar_entries = entries(list_tile, SCALAR_HALF * HALF, HALF)
+                vector_entries = entries(list_tile, VECTOR_HALF * HALF, HALF)
+                nc.scalar.activation(picked[SCALAR_HALF][:, t, :], window.indirect(scalar_entries), COPY)
+                nc.vector.tensor_copy(picked[VECTOR_HALF][:, t, :], window.indirect(vector_entries))
+
+        def weave(copy, woven, picked):
+            copy(woven[:].rearrange("p (c i) t -> p c t i", i=4), picked[:].rearrange("p t (c i) -> p c t i", i=4))
 
         def quantise(codes, scales, woven):
             nc.vector.quantize_mx(out=codes.bitcast(FP8X4), scales=scales, in_=woven[:].rearrange("p j t -> p (j t)"))
 
         key_scales = sb.tile([P, I], U8, name="key_scales", align_bytes=64)
         nc.vector.tensor_copy(key_scales[:], key_scale_pool[:].indirect(key_list[:]))
+
         note_picked = [
             sb.tile([P, PACK, HALF], BF16, name="note_picked0"),
-            sb.tile([P, PACK, HALF], BF16, name="note_picked1"),
+            reused_tile([P, PACK, HALF], BF16, "note_picked1", SCALAR_PICKED_AT),
         ]
-        note_woven = gather_and_weave("note", note_planes, note_list, note_picked, [(t, 1) for t in range(PACK)])
+        gather_planes(note_planes, note_list, note_picked)
+        note_woven = [
+            sb.tile([P, HALF, PACK], BF16, name="note_woven0", align_bytes=64),
+            reused_tile([P, HALF, PACK], BF16, "note_woven1", NOTE_WOVEN_AT),
+        ]
+        weave(nc.vector.tensor_copy, note_woven[VECTOR_HALF], note_picked[VECTOR_HALF])
+        weave(nc.scalar.copy, note_woven[SCALAR_HALF], note_picked[SCALAR_HALF])
         note_codes = sb.tile([P, J], U32, name="note_codes", align_bytes=64)
         note_scales = sb.tile([P, J], U8, name="note_scales", align_bytes=64)
         for h in range(2):
@@ -125,81 +139,90 @@ def tile_attend_tab_larger_keep_kernel(tc, keys_words, keys_scales, notes, users
         key_words = sb.tile([P, I], U32, name="key_words", align_bytes=64)
         nc.vector.tensor_copy(key_words[:], key_word_pool[:].bitcast(U32).indirect(key_list[:]))
 
-        def product(bank, r, codes, scales):
+        def product(bank_columns, r, codes, scales):
             rows = slice(r * P, (r + 1) * P)
             nc.tensor.matmul_mx(
-                out=bank, lhsT=key_words[:, rows].bitcast(FP8X4), lhsT_scale=key_scales[:, rows],
-                rhs=codes.bitcast(FP8X4), rhs_scale=scales, start=True, stop=True,
+                out=bank_columns,
+                lhsT=key_words[:, rows].bitcast(FP8X4),
+                lhsT_scale=key_scales[:, rows],
+                rhs=codes.bitcast(FP8X4),
+                rhs_scale=scales,
+                start=True,
+                stop=True,
             )
 
-        g1_banks = []
+        g1_banks = [ps.tile([P, J], F32, name="g1_bank%d" % r, tag="g1_%d" % r) for r in range(ROW_TILES)]
         for r in range(ROW_TILES):
-            bank = ps.tile([P, J], F32, name="g1_bank%d" % r, tag="first%d" % r)
-            product(bank[:], r, note_codes[:], note_scales[:])
-            g1_banks.append(bank)
+            product(g1_banks[r][:], r, note_codes[:], note_scales[:])
 
-        g1 = []
         user_picked = [
-            reuse.tile([P, PACK, HALF], BF16, name="user_picked0", align_bytes=64, offset=4 * T - 1024),
-            reuse.tile([P, PACK, HALF], BF16, name="user_picked1", align_bytes=64, offset=4 * T + 1024),
+            reused_tile([P, PACK, HALF], BF16, "user_picked0", USER_PICKED_AT),
+            reused_tile([P, PACK, HALF], BF16, "user_picked1", SCALAR_PICKED_AT),
         ]
-        user_woven = gather_and_weave("user", user_planes, user_list, user_picked, [(0, 0), (0, 1), (3, 1)])
+        gather_planes(user_planes, user_list, user_picked)
+        user_woven = [sb.tile([P, HALF, PACK], BF16, name="user_woven%d" % h, align_bytes=64) for h in range(2)]
+        for h in range(2):
+            weave(nc.vector.tensor_copy, user_woven[h], user_picked[h])
+
+        g1 = reused_tile([P, ROW_TILES * J], F32, "g1", LAST_PLANES_AT)
         for r in range(ROW_TILES):
-            t = sb.tile([P, J], F32, name="g1_%d" % r)
-            nc.scalar.copy(t[:], g1_banks[r][:])
-            g1.append(t)
+            nc.scalar.copy(g1[:, r * J : (r + 1) * J], g1_banks[r][:])
+
+        g2_banks = [ps.tile([P, J], F32, name="g2_bank%d" % r, tag="g2_%d" % r) for r in range(ROW_TILES)]
+        user_codes = [sb.tile([P, HALF], U32, name="user_codes%d" % h, align_bytes=64) for h in range(2)]
+        user_scales = [sb.tile([P, HALF], U8, name="user_scales%d" % h, align_bytes=64) for h in range(2)]
+        quantise(user_codes[0][:], user_scales[0][:], user_woven[0])
+        for r in range(ROW_TILES):
+            product(g2_banks[r][:, :HALF], r, user_codes[0][:], user_scales[0][:])
+        quantise(user_codes[1][:], user_scales[1][:], user_woven[1])
+        g2_spare_bank = ps.tile([P, J], F32, name="g2_spare_bank", tag="g1_0")
+        product(g2_spare_bank[:, HALF:], 0, user_codes[1][:], user_scales[1][:])
+        for r in range(1, ROW_TILES):
+            product(g2_banks[r][:, HALF:], r, user_codes[1][:], user_scales[1][:])
 
         g0 = [sb.tile([P, J], F32, name="g0_%d" % r) for r in range(ROW_TILES)]
-        g2_banks = {}
 
-        def users_half(h):
-            codes = sb.tile([P, HALF], U32, name="user_codes%d" % h, align_bytes=64)
-            scales = sb.tile([P, HALF], U8, name="user_scales%d" % h, align_bytes=64)
-            quantise(codes[:], scales[:], user_woven[h])
-            for r in range(ROW_TILES):
-                bank = ps.tile([P, J], F32, name="g2_bank%d_%d" % (r, h), tag=("second%d" if h == 0 else "first%d") % r)
-                product(bank[:, :HALF], r, codes[:], scales[:])
-                g2_banks[(r, h)] = bank
+        def larger(r, bank, first, count):
+            cols = slice(first, first + count)
+            g1_cols = slice(r * J + first, r * J + first + count)
+            nc.vector.tensor_tensor(g0[r][:, cols], bank[:, cols], g1[:, g1_cols], ALU.max)
 
-        def larger(r, h):
-            cols = slice(h * HALF, (h + 1) * HALF)
-            nc.vector.tensor_tensor(g0[r][:, cols], g2_banks[(r, h)][:, :HALF], g1[r][:, cols], ALU.max)
+        def place_on_vector(r, first, count):
+            window = placed[r][:].indirect(entries(place_list, first, count))
+            nc.vector.tensor_copy(window, g0[r][:, first : first + count])
 
-        def place_vector(r, first, count):
-            nc.vector.tensor_copy(placed[r][:].indirect(entries(place_list, first, count)), g0[r][:, first : first + count])
-
-        def place_scalar(r, first, count):
-            nc.scalar.activation(placed[r][:].indirect(entries(place_list, first, count)), g0[r][:, first : first + count], COPY)
+        def place_on_scalar(r, first, count):
+            window = placed[r][:].indirect(entries(place_list, first, count))
+            nc.scalar.activation(window, g0[r][:, first : first + count], COPY)
 
         def finish(r, pieces):
             width = M // pieces
             for k in range(pieces):
                 cols = slice(k * width, (k + 1) * width)
                 nc.vector.scalar_tensor_tensor(
-                    out=old_sb[r][:, cols], in0=old_sb[r][:, cols], scalar=fade_sb[:, r : r + 1],
-                    in1=placed[r][:, cols], op0=ALU.mult, op1=ALU.add,
+                    out=old_tiles[r][:, cols],
+                    in0=old_tiles[r][:, cols],
+                    scalar=fade_columns[:, r : r + 1],
+                    in1=placed[r][:, cols],
+                    op0=ALU.mult,
+                    op1=ALU.add,
                 )
-                nc.sync.dma_start(out[r * P : (r + 1) * P, cols], old_sb[r][:, cols])
+                nc.sync.dma_start(out[r * P : (r + 1) * P, cols], old_tiles[r][:, cols])
 
-        users_half(0)
-        larger(0, 0)
-        place_scalar(0, 0, HALF)
-        users_half(1)
-        larger(0, 1)
-        place_scalar(0, HALF, HALF)
-        larger(1, 0)
-        larger(1, 1)
-        place_scalar(1, 0, HALF)
-        place_scalar(1, HALF, HALF)
-        larger(3, 0)
-        larger(3, 1)
-        place_vector(3, 0, HALF)
-        larger(2, 0)
-        larger(2, 1)
-        place_vector(3, HALF, HALF)
-        place_vector(2, 384, 128)
-        place_scalar(2, 0, 384)
+        larger(0, g2_banks[0], 0, HALF)
+        place_on_scalar(0, 0, HALF)
+        larger(0, g2_spare_bank, HALF, HALF)
+        place_on_scalar(0, HALF, HALF)
+        larger(1, g2_banks[1], 0, J)
+        place_on_scalar(1, 0, HALF)
+        place_on_scalar(1, HALF, HALF)
+        larger(2, g2_banks[2], 0, J)
+        place_on_vector(2, 0, J)
+        larger(3, g2_banks[3], 0, J)
+        place_on_vector(3, LAST_TILE_ON_SCALAR, J - LAST_TILE_ON_SCALAR)
+        place_on_scalar(3, 0, LAST_TILE_ON_SCALAR)
+
         finish(0, 1)
-        finish(3, 1)
+        finish(2, 1)
         finish(1, 1)
-        finish(2, 2)
+        finish(3, 2)

from contextlib import ExitStack

import concourse.mybir as mybir
from concourse.masks import make_identity

D, T, I, J, U, M = 512, 2048, 512, 512, 1024, 1024
FLOPS = 2 * 2 * D * I * J

F32 = mybir.dt.float32
BF16 = mybir.dt.bfloat16
I32 = mybir.dt.int32
U32 = mybir.dt.uint32
U16 = mybir.dt.uint16
U8 = mybir.dt.uint8
FP8X4 = mybir.dt.float8_e4m3fn_x4
COPY = mybir.ActivationFunctionType.Copy
ALU = mybir.AluOpType

P = 128
PACK = 4
QUADRANTS = 4
ROW_TILES = I // P
HALF = J // 2
ENTRIES_PER_COLUMN = 16
VECTOR_HALF, SCALAR_HALF = 0, 1

LAST_TILE_ON_SCALAR = 384

KIB = 1024
KEY_WORDS_AT = 0
NOTE_WOVEN_AT = 8 * KIB
USER_PICKED_AT = 7 * KIB
SCALAR_PICKED_AT = 11 * KIB
LAST_PLANES_AT = 14 * KIB


def tile_attend_tab_larger_keep_kernel(tc, keys_words, keys_scales, notes, users2, old, fade, offs, offs2, offs3, offs4, out):
    nc = tc.nc
    with ExitStack() as ctx:
        sb = ctx.enter_context(tc.tile_pool(name="sb", bufs=1))
        reuse = ctx.enter_context(tc.tile_pool(name="reuse", bufs=1))
        ps = ctx.enter_context(tc.psum_pool(name="ps", bufs=1))

        def reused_tile(shape, dtype, name, offset):
            return reuse.tile(shape, dtype, name=name, align_bytes=64, offset=offset)

        def load_list(name, source):
            list_tile = sb.tile([P, source.shape[1]], U16, name=name)
            nc.sync.dma_start(list_tile[:], source)
            return list_tile

        def entries(list_tile, first, count):
            return list_tile[:, first // ENTRIES_PER_COLUMN : (first + count) // ENTRIES_PER_COLUMN]

        note_rows = notes.rearrange("(p t) u -> t p u", t=PACK)
        note_planes = [sb.tile([P, U], F32, name="note_plane%d" % t) for t in range(PACK)]
        for h in range(2):
            cols = slice(h * U // 2, (h + 1) * U // 2)
            nc.sync.dma_start(note_planes[0][:, cols], note_rows[0][:, cols])
        note_list = load_list("note_list", offs2)
        key_list = load_list("key_list", offs)
        user_list = load_list("user_list", offs3)
        place_list = load_list("place_list", offs4)
        for t in (1, 2):
            nc.sync.dma_start(note_planes[t][:], note_rows[t])

        key_scale_pool = sb.tile([P, T], U8, name="key_scale_pool", align_bytes=64)
        nc.gpsimd.memset(key_scale_pool[:].bitcast(I32), 0)
        for q in range(QUADRANTS):
            nc.sync.dma_start(
                key_scale_pool[32 * q : 32 * q + 4, :].bitcast(I32),
                keys_scales[0, 4 * q : 4 * q + 4, :].bitcast(I32),
            )
        fade_rows = sb.tile([P, P], F32, name="fade_rows")
        nc.gpsimd.memset(fade_rows[:], 0.0)
        nc.sync.dma_start(fade_rows[0:ROW_TILES, :], fade.rearrange("(r p) o -> r (p o)", p=P))
        nc.sync.dma_start(note_planes[3][:], note_rows[3])

        key_word_pool = reused_tile([P, T], I32, "key_word_pool", KEY_WORDS_AT)
        nc.sync.dma_start(key_word_pool[:], keys_words[0].rearrange("p c r -> p (c r)").bitcast(I32))

        user_rows = users2.rearrange("(p t) u -> t p u", t=PACK)
        user_planes = [sb.tile([P, U], F32, name="user_plane%d" % t) for t in (0, 1)]
        user_planes.extend(
            reused_tile([P, U], F32, "user_plane%d" % t, LAST_PLANES_AT + (t - 2) * 4 * U) for t in (2, 3)
        )
        for t in range(PACK):
            nc.sync.dma_start(user_planes[t][:], user_rows[t])

        old_tiles = [sb.tile([P, M], F32, name="old%d" % r) for r in range(ROW_TILES)]
        for r in range(ROW_TILES):
            nc.sync.dma_start(old_tiles[r][:], old[r * P : (r + 1) * P, :])

        placed = [sb.tile([P, M], F32, name="placed%d" % r) for r in range(ROW_TILES)]
        for r in range(ROW_TILES):
            nc.vector.memset(placed[r][:].bitcast(I32), 0)

        identity = sb.tile([P, P], F32, name="identity")
        make_identity(nc, identity[:])
        fade_bank = ps.tile([P, P], F32, name="fade_bank", tag="g2_3")
        nc.tensor.transpose(fade_bank[:], fade_rows[:], identity[:])
        fade_columns = sb.tile([P, ROW_TILES], F32, name="fade_columns")
        nc.scalar.copy(fade_columns[:], fade_bank[:, :ROW_TILES])

        def gather_planes(planes, list_tile, picked):
            for t in range(PACK):
                window = planes[t][:]
                scalar_entries = entries(list_tile, SCALAR_HALF * HALF, HALF)
                vector_entries = entries(list_tile, VECTOR_HALF * HALF, HALF)
                nc.scalar.activation(picked[SCALAR_HALF][:, t, :], window.indirect(scalar_entries), COPY)
                nc.vector.tensor_copy(picked[VECTOR_HALF][:, t, :], window.indirect(vector_entries))

        def weave(copy, woven, picked):
            copy(woven[:].rearrange("p (c i) t -> p c t i", i=4), picked[:].rearrange("p t (c i) -> p c t i", i=4))

        def quantise(codes, scales, woven):
            nc.vector.quantize_mx(out=codes.bitcast(FP8X4), scales=scales, in_=woven[:].rearrange("p j t -> p (j t)"))

        key_scales = sb.tile([P, I], U8, name="key_scales", align_bytes=64)
        nc.vector.tensor_copy(key_scales[:], key_scale_pool[:].indirect(key_list[:]))

        note_picked = [
            sb.tile([P, PACK, HALF], BF16, name="note_picked0"),
            reused_tile([P, PACK, HALF], BF16, "note_picked1", SCALAR_PICKED_AT),
        ]
        gather_planes(note_planes, note_list, note_picked)
        note_woven = [
            sb.tile([P, HALF, PACK], BF16, name="note_woven0", align_bytes=64),
            reused_tile([P, HALF, PACK], BF16, "note_woven1", NOTE_WOVEN_AT),
        ]
        weave(nc.vector.tensor_copy, note_woven[VECTOR_HALF], note_picked[VECTOR_HALF])
        weave(nc.scalar.copy, note_woven[SCALAR_HALF], note_picked[SCALAR_HALF])
        note_codes = sb.tile([P, J], U32, name="note_codes", align_bytes=64)
        note_scales = sb.tile([P, J], U8, name="note_scales", align_bytes=64)
        for h in range(2):
            cols = slice(h * HALF, (h + 1) * HALF)
            quantise(note_codes[:, cols], note_scales[:, cols], note_woven[h])

        key_words = sb.tile([P, I], U32, name="key_words", align_bytes=64)
        nc.vector.tensor_copy(key_words[:], key_word_pool[:].bitcast(U32).indirect(key_list[:]))

        def product(bank_columns, r, codes, scales):
            rows = slice(r * P, (r + 1) * P)
            nc.tensor.matmul_mx(
                out=bank_columns,
                lhsT=key_words[:, rows].bitcast(FP8X4),
                lhsT_scale=key_scales[:, rows],
                rhs=codes.bitcast(FP8X4),
                rhs_scale=scales,
                start=True,
                stop=True,
            )

        g1_banks = [ps.tile([P, J], F32, name="g1_bank%d" % r, tag="g1_%d" % r) for r in range(ROW_TILES)]
        for r in range(ROW_TILES):
            product(g1_banks[r][:], r, note_codes[:], note_scales[:])

        user_picked = [
            reused_tile([P, PACK, HALF], BF16, "user_picked0", USER_PICKED_AT),
            reused_tile([P, PACK, HALF], BF16, "user_picked1", SCALAR_PICKED_AT),
        ]
        gather_planes(user_planes, user_list, user_picked)
        user_woven = [sb.tile([P, HALF, PACK], BF16, name="user_woven%d" % h, align_bytes=64) for h in range(2)]
        for h in range(2):
            weave(nc.vector.tensor_copy, user_woven[h], user_picked[h])

        g1 = reused_tile([P, ROW_TILES * J], F32, "g1", LAST_PLANES_AT)
        for r in range(ROW_TILES):
            nc.scalar.copy(g1[:, r * J : (r + 1) * J], g1_banks[r][:])

        g2_banks = [ps.tile([P, J], F32, name="g2_bank%d" % r, tag="g2_%d" % r) for r in range(ROW_TILES)]
        user_codes = [sb.tile([P, HALF], U32, name="user_codes%d" % h, align_bytes=64) for h in range(2)]
        user_scales = [sb.tile([P, HALF], U8, name="user_scales%d" % h, align_bytes=64) for h in range(2)]
        quantise(user_codes[0][:], user_scales[0][:], user_woven[0])
        for r in range(ROW_TILES):
            product(g2_banks[r][:, :HALF], r, user_codes[0][:], user_scales[0][:])
        quantise(user_codes[1][:], user_scales[1][:], user_woven[1])
        g2_spare_bank = ps.tile([P, J], F32, name="g2_spare_bank", tag="g1_0")
        product(g2_spare_bank[:, HALF:], 0, user_codes[1][:], user_scales[1][:])
        for r in range(1, ROW_TILES):
            product(g2_banks[r][:, HALF:], r, user_codes[1][:], user_scales[1][:])

        g0 = [sb.tile([P, J], F32, name="g0_%d" % r) for r in range(ROW_TILES)]

        def larger(r, bank, first, count):
            cols = slice(first, first + count)
            g1_cols = slice(r * J + first, r * J + first + count)
            nc.vector.tensor_tensor(g0[r][:, cols], bank[:, cols], g1[:, g1_cols], ALU.max)

        def place_on_vector(r, first, count):
            window = placed[r][:].indirect(entries(place_list, first, count))
            nc.vector.tensor_copy(window, g0[r][:, first : first + count])

        def place_on_scalar(r, first, count):
            window = placed[r][:].indirect(entries(place_list, first, count))
            nc.scalar.activation(window, g0[r][:, first : first + count], COPY)

        def finish(r, pieces):
            width = M // pieces
            for k in range(pieces):
                cols = slice(k * width, (k + 1) * width)
                nc.vector.scalar_tensor_tensor(
                    out=old_tiles[r][:, cols],
                    in0=old_tiles[r][:, cols],
                    scalar=fade_columns[:, r : r + 1],
                    in1=placed[r][:, cols],
                    op0=ALU.mult,
                    op1=ALU.add,
                )
                nc.sync.dma_start(out[r * P : (r + 1) * P, cols], old_tiles[r][:, cols])

        larger(0, g2_banks[0], 0, HALF)
        place_on_scalar(0, 0, HALF)
        larger(0, g2_spare_bank, HALF, HALF)
        place_on_scalar(0, HALF, HALF)
        larger(1, g2_banks[1], 0, J)
        place_on_scalar(1, 0, HALF)
        place_on_scalar(1, HALF, HALF)
        larger(2, g2_banks[2], 0, J)
        place_on_vector(2, 0, J)
        larger(3, g2_banks[3], 0, J)
        place_on_vector(3, LAST_TILE_ON_SCALAR, J - LAST_TILE_ON_SCALAR)
        place_on_scalar(3, 0, LAST_TILE_ON_SCALAR)

        finish(0, 1)
        finish(2, 1)
        finish(1, 1)
        finish(3, 2)
